import numpy as np
import ml_dtypes


def mxq(x, axis, fmt="e4m3"):
    dtype, down = {"e4m3": (ml_dtypes.float8_e4m3fn, 7), "e5m2": (ml_dtypes.float8_e5m2, 14)}[fmt]
    v = np.moveaxis(np.asarray(x, np.float32).astype(ml_dtypes.bfloat16).astype(np.float64), axis, -1)
    blocks = v.reshape(v.shape[:-1] + (-1, 32))
    amax = np.abs(blocks).max(-1, keepdims=True)
    byte = np.maximum(np.where(amax > 0, np.frexp(amax)[1] - 1 + 127, 0) - down, 1)
    scale = np.exp2(byte - 127.0)
    codes = (blocks / scale).astype(np.float32).astype(dtype).astype(np.float64)
    return np.moveaxis((codes * scale).reshape(v.shape), -1, axis)


WIDE = False


def mx_kscale(k):
    if not WIDE:
        return np.ones(k)
    levels = np.array([10, -10, 5, -5, 0])
    if k % 512:
        return np.exp2(np.random.permutation(np.resize(levels, k // 32))).repeat(32)
    a = np.empty((k // 512, 16))
    for p in range(k // 512):
        a[p, :8] = np.random.permutation(np.resize(levels, 8))
        for g in range(8):
            far = levels[np.abs(levels - a[p, g]) >= 10]
            a[p, g + 8] = far[np.random.randint(len(far))]
    return np.exp2(a.ravel()).repeat(32)


def f64(x):
    return np.asarray(x).astype(np.float64)


def striped(idx):
    return np.tile(idx.reshape(-1, 16).T, (8, 1)).astype(np.uint16)


def unstriped(offs):
    return offs[:16].T.reshape(-1).astype(np.int64)


E2M1 = np.array([0.0, 0.5, 1.0, 1.5, 2.0, 3.0, 4.0, 6.0, -0.0, -0.5, -1.0, -1.5, -2.0, -3.0, -4.0, -6.0])


def pack_weight(w, fmt):
    k, n = w.shape
    w = f64(np.asarray(w, np.float32).astype(ml_dtypes.bfloat16)).reshape(k // 32, 32, n)
    amax = np.abs(w).max(1)
    if fmt == "e4m3":
        byte = np.frexp(amax)[1] - 1 + 127 - 7
    else:
        mant, ex = np.frexp(amax / 6.0)
        byte = np.where(mant > 0.5, ex, ex - 1) + 127
    byte = np.clip(np.where(amax > 0, byte, 1), 1, 254)
    scaled = (w * np.exp2(127.0 - byte)[:, None, :]).reshape(k, n).astype(np.float32)
    by_word = np.ascontiguousarray(scaled.reshape(k // 512, 128, 4, n).transpose(0, 1, 3, 2))
    if fmt == "e4m3":
        words = by_word.astype(ml_dtypes.float8_e4m3fn).view(np.uint8)
    else:
        c = by_word.astype(ml_dtypes.float4_e2m1fn).view(np.uint8) & 0xF
        words = (c[..., 0::2] | (c[..., 1::2] << 4)).reshape(k // 512, 128, 2 * n)
    return np.ascontiguousarray(words), np.ascontiguousarray(byte.astype(np.uint8).reshape(k // 512, 16, n))


def unpack_weight(words, scales, fmt):
    g, _, n = scales.shape
    words = np.ascontiguousarray(words).reshape(g, 128, n, -1)
    if fmt == "e4m3":
        vals = words.view(ml_dtypes.float8_e4m3fn).astype(np.float64)
    else:
        nib = np.empty((g, 128, n, 4), np.uint8)
        nib[..., 0::2] = words & 0xF
        nib[..., 1::2] = words >> 4
        vals = E2M1[nib]
    vals = vals * np.repeat(np.exp2(scales.astype(np.float64) - 127.0), 8, axis=1)[..., None]
    return vals.transpose(0, 1, 3, 2).reshape(g * 512, n)


def gelu(v):
    return 0.5 * v * (1.0 + np.tanh(np.sqrt(2.0 / np.pi) * (v + 0.044715 * v**3)))


def bf(x):
    return np.asarray(x, np.float32).astype(ml_dtypes.bfloat16)


def planes(Y):
    n, m = Y.shape
    b = f64(bf(Y)).reshape(n // 32, 32, m)
    amax = np.abs(b).max(1)
    byte = np.clip(np.where(amax > 0, np.frexp(amax)[1] - 1 + 127 - 7, 1), 1, 254)
    codes = (b * np.exp2(127.0 - byte)[:, None, :]).reshape(n, m).astype(np.float32).astype(ml_dtypes.float8_e4m3fn).view(np.uint8)
    words = codes.reshape(n // 512, 128, 4, m).transpose(0, 1, 3, 2)
    return np.ascontiguousarray(words), np.ascontiguousarray(byte.astype(np.uint8).reshape(n // 512, 16, m))


K, T, S, H, T2, P, N = 1536, 2048, 1024, 512, 2048, 1024, 512

def setup_inputs():
    n = np.random.standard_normal
    s = mx_kscale(K)[:, None]
    u = mx_kscale(H)[:, None]
    d = {}
    d["tab_words"], d["tab_scales"] = pack_weight(n((K, T)) * s, "e4m3")
    d["offs"] = striped(np.random.permutation(T)[:S])
    d["w1"] = (n((K, H)) / K ** 0.5 / s).astype(np.float32)
    d["vec"] = (np.exp(0.3 * n(H)) * u[:, 0]).astype(np.float32)
    d["weather"] = (0.7 * n((H, S)) * u).astype(np.float32)
    d["wgs"] = np.exp(0.3 * n((128, S))).astype(np.float32)
    d["page0"] = (n((H, T2)) * u).astype(np.float32)
    d["offs2"] = striped(np.random.permutation(T2)[:S])
    d["offs3"] = striped(np.random.permutation(T2)[:P])
    d["sat"] = ((0.3 + 0.9 * n((H, P))) * u).astype(np.float32)
    d["w3"] = (n((H, N)) / H ** 0.5 / u).astype(np.float32)
    d["w4_words"], d["w4_scales"] = pack_weight(n((H, N)) / H ** 0.5 / u, "e2m1")
    d["sluice"] = n((N, P)).astype(np.float32)
    return d

def reference(tab_words, tab_scales, offs, w1, vec, weather, wgs, page0, offs2, offs3, sat, w3, w4_words, w4_scales, sluice):
    v = unpack_weight(tab_words, tab_scales, "e4m3")[:, unstriped(offs)]
    b = mxq(f64(w1), 0, "e4m3").T @ v
    h = f64(vec)[:, None] * b + f64(weather)
    page = f64(page0).copy()
    page[:, unstriped(offs2)] = np.tile(f64(wgs), (H // 128, 1)) * h
    x = np.minimum(page[:, unstriped(offs3)], f64(sat))
    xq = mxq(x, 0, "e4m3")
    y1 = unpack_weight(w4_words, w4_scales, "e2m1").T @ xq
    y2 = mxq(f64(w3), 0, "e4m3").T @ xq
    y = y1 + f64(sluice) * y2
    words, scales = planes(page)
    return y, page, words, scales

@@ -1,0 +1,221 @@
+from contextlib import ExitStack
+
+import concourse.mybir as mybir
+from concourse.masks import make_identity
+
+K, T, S, H, T2, M, N = 1536, 2048, 1024, 512, 2048, 1024, 512
+FLOPS = 2 * K * H * S + 2 * 2 * H * N * M
+
+F32 = mybir.dt.float32
+BF16 = mybir.dt.bfloat16
+I32 = mybir.dt.int32
+U32 = mybir.dt.uint32
+U16 = mybir.dt.uint16
+U8 = mybir.dt.uint8
+FP8X4 = mybir.dt.float8_e4m3fn_x4
+FP4X4 = mybir.dt.float4_e2m1fn_x4
+MULT = mybir.AluOpType.mult
+ADD = mybir.AluOpType.add
+MIN = mybir.AluOpType.min
+
+P = 128
+PACK = 4
+BANK = 512
+PASSES = K // (P * PACK)
+ALIGN = 64
+
+
+def tile_list_brine_pond_page_kernel(
+    tc, tab_words, tab_scales, offs, w1, vec, weather, wgs, page0, offs2, offs3, sat, w3, w4_words, w4_scales, sluice,
+    out_0, out_1, out_2, out_3,
+):
+    nc = tc.nc
+    with ExitStack() as ctx:
+        lists = ctx.enter_context(tc.tile_pool(name="lists", bufs=1))
+        keep = ctx.enter_context(tc.tile_pool(name="keep", bufs=1))
+        ring = ctx.enter_context(tc.tile_pool(name="ring", bufs=2))
+        psum = ctx.enter_context(tc.psum_pool(name="psum", bufs=4))
+
+        def held(shape, dtype, name, tag=None):
+            return keep.tile(shape, dtype, name=name, tag=tag or name, align_bytes=ALIGN)
+
+        pick = lists.tile([P, S // 16], U16, name="pick")
+        put = lists.tile([P, S // 16], U16, name="put")
+        fetch = lists.tile([P, M // 16], U16, name="fetch")
+
+        tab_sc = held([P, T], U8, "tab_sc")
+        nc.vector.memset(tab_sc[:].bitcast(I32), 0)
+        for q in range(4):
+            nc.scalar.dma_start(
+                tab_sc[32 * q : 32 * q + 4 * PASSES, :].bitcast(I32), tab_scales[:, 4 * q : 4 * q + 4, :].bitcast(I32)
+            )
+        wgs_rows = held([P, S], F32, "wgs_rows")
+        nc.sync.dma_start(pick[:], offs)
+        nc.sync.dma_start(wgs_rows[:], wgs)
+        tab = [held([P, T], I32, "tab%d" % a, "slot_a%d" % a) for a in range(PASSES)]
+        w1_raw = [held([P, PACK, H], F32, "w1_raw%d" % a, "slot_b%d" % a) for a in range(PASSES)]
+        for a in range(PASSES):
+            nc.sync.dma_start(tab[a][:], tab_words[a].rearrange("p t i -> p (t i)").bitcast(I32))
+            nc.sync.dma_start(w1_raw[a][:], w1[512 * a : 512 * (a + 1), :].rearrange("(p j) r -> p j r", j=PACK))
+
+        ident = held([P, P], F32, "ident")
+        make_identity(nc, ident[:])
+        vec_sb = held([P, PACK], F32, "vec_sb")
+        nc.gpsimd.dma_start(vec_sb[:], vec.rearrange("(p t) -> p t", t=PACK))
+        w4_sc = held([P, N], U8, "w4_sc")
+        nc.gpsimd.memset(w4_sc[:].bitcast(I32), 0)
+        for q in range(4):
+            nc.gpsimd.dma_start(w4_sc[32 * q : 32 * q + 4, :].bitcast(I32), w4_scales[0, 4 * q : 4 * q + 4, :].bitcast(I32))
+
+        weather_rows = weather.rearrange("(p t) j -> t p j", t=PACK)
+        page_rows = page0.rearrange("(p t) c -> t p c", t=PACK)
+        wea = [held([P, S], F32, "wea%d" % t, "slot_c%d" % t) for t in range(PACK)]
+        page = [held([P, T2], F32, "page%d" % t) for t in range(PACK)]
+        nc.sync.dma_start(put[:], offs2)
+        for t in range(PACK):
+            nc.sync.dma_start(wea[t][:], weather_rows[t])
+            nc.sync.dma_start(page[t][:], page_rows[t])
+
+        wgs_t = [held([P, 4, PACK, 4, 32], F32, "wgs_t%d" % u, "slot_e%d" % u) for u in range(S // BANK)]
+        for half in range(S // BANK):
+            bank = psum.tile([P, 4, P], F32, name="bank", tag="plain")
+            for b in range(4):
+                j0 = BANK * half + P * b
+                nc.tensor.transpose(bank[:, b, :], wgs_rows[:, j0 : j0 + P], ident[:])
+            for b in range(4):
+                src = bank[:, b, :].rearrange("j (q t) -> j t q", t=PACK).unsqueeze(2).to_broadcast([P, PACK, 4, 32])
+                nc.scalar.copy(wgs_t[half][:, b, :, :, :], src)
+        wgd = [held([P, S], F32, "wgd%d" % t) for t in range(PACK)]
+
+        def deal_wgs(t):
+            for half in range(S // BANK):
+                bank = psum.tile([P, 4, P], F32, name="bank", tag="plain")
+                for b in range(4):
+                    nc.tensor.transpose(
+                        bank[:, b, :], wgs_t[half][:, b, t, :, :].rearrange("j g q -> j (g q)"), ident[:]
+                    )
+                nc.scalar.copy(wgd[t][:, BANK * half : BANK * (half + 1)], bank[:].rearrange("p b j -> p (b j)"))
+
+        deal_wgs(0)
+
+        v_words = [held([P, S], U32, "v_words%d" % a) for a in range(PASSES)]
+        v_sc = held([P, S], U8, "v_sc")
+        w1_q = [held([P, H], U32, "w1_q%d" % a) for a in range(PASSES)]
+        w1_sc = [held([P, H], U8, "w1_sc%d" % a) for a in range(PASSES)]
+        for a in range(PASSES):
+            nc.vector.tensor_copy(v_words[a][:], tab[a][:].bitcast(U32).indirect(pick[:]))
+            if a == 0:
+                nc.vector.tensor_copy(v_sc[:], tab_sc[:].indirect(pick[:]))
+            dealt = w1_raw[a][:].rearrange("p j (m t) -> p m t j", t=PACK)
+            if a < PASSES - 1:
+                grouped = held([P, PACK, P, PACK], BF16, "w1_bf%d" % a, "slot_d%d" % a)
+                nc.scalar.copy(grouped[:].rearrange("p t m j -> p m t j"), dealt)
+                nc.vector.quantize_mx(w1_q[a][:].bitcast(FP8X4), w1_sc[a][:], grouped[:].rearrange("p t m j -> p (t m j)"))
+            else:
+                first = held([P, P, PACK], BF16, "w1_bf_first")
+                nc.vector.tensor_copy(first[:], dealt[:, :, 0, :])
+                nc.vector.quantize_mx(
+                    w1_q[a][:, 0:P].bitcast(FP8X4), w1_sc[a][:, 0:P], first[:].rearrange("p m j -> p (m j)")
+                )
+                rest = held([P, PACK - 1, P, PACK], BF16, "w1_bf_rest")
+                nc.scalar.copy(rest[:].rearrange("p t m j -> p m t j"), dealt[:, :, 1:PACK, :])
+                for t in range(1, PACK):
+                    cols = slice(P * t, P * (t + 1))
+                    nc.vector.quantize_mx(
+                        w1_q[a][:, cols].bitcast(FP8X4), w1_sc[a][:, cols], rest[:, t - 1, :, :].rearrange("p m j -> p (m j)")
+                    )
+        for t in range(1, PACK):
+            deal_wgs(t)
+
+        chunks = M // BANK
+        nc.sync.dma_start(fetch[:], offs3)
+        w3_raw = held([P, PACK, N], F32, "w3_raw", "slot_a2")
+        nc.sync.dma_start(w3_raw[:], w3.rearrange("(p j) n -> p j n", j=PACK))
+        w4_q = held([P, 2 * N], U8, "w4_q")
+        nc.sync.dma_start(w4_q[:].bitcast(I32), w4_words[0].bitcast(I32))
+        sat_sb = [held([P, PACK, BANK], F32, "sat%d" % c, "slot_a%d" % c) for c in range(chunks)]
+        slu = [held([P, N // P, BANK], F32, "slu%d" % c, "slot_b%d" % c) for c in range(chunks)]
+        for c in range(chunks):
+            cols = slice(BANK * c, BANK * (c + 1))
+            nc.sync.dma_start(sat_sb[c][:], sat[:, cols].rearrange("(p t) m -> p t m", t=PACK))
+            nc.sync.dma_start(slu[c][:], sluice[:, cols].rearrange("(b p) m -> p b m", p=P))
+
+        out_rows = out_1.rearrange("(p t) c -> t p c", t=PACK)
+        page_bf = [
+            held([P, PACK, T2 // 2], BF16, "page_bf0", "slot_b2"),
+            held([P, PACK, T2 // 2], BF16, "page_bf1"),
+        ]
+        for t in range(PACK):
+            h = ring.tile([P, S], F32, name="h")
+            rows = slice(P * t, P * (t + 1))
+            for half in range(S // BANK):
+                cols = slice(BANK * half, BANK * (half + 1))
+                acc = psum.tile([P, BANK], F32, name="acc", tag="mx")
+                for a in range(PASSES):
+                    nc.tensor.matmul_mx(
+                        acc[:], lhsT=w1_q[a][:, rows].bitcast(FP8X4), lhsT_scale=w1_sc[a][:, rows],
+                        rhs=v_words[a][:, cols].bitcast(FP8X4), rhs_scale=v_sc[4 * a : P, cols],
+                        start=(a == 0), stop=(a == PASSES - 1),
+                    )
+                nc.vector.scalar_tensor_tensor(h[:, cols], acc[:], vec_sb[:, t : t + 1], wea[t][:, cols], MULT, ADD)
+            nc.vector.tensor_tensor(page[t][:].indirect(put[:]), h[:], wgd[t][:], MULT)
+            nc.sync.dma_start(out_rows[t], page[t][:])
+            for u in range(2):
+                nc.scalar.copy(page_bf[u][:, t, :], page[t][:, 1024 * u : 1024 * (u + 1)])
+
+        w3_bf = held([P, N, PACK], BF16, "w3_bf", "slot_d0")
+        nc.scalar.copy(
+            w3_bf[:].rearrange("p (c i) j -> p c j i", i=4), w3_raw[:].rearrange("p j (c i) -> p c j i", i=4)
+        )
+        w3_q = held([P, N], U32, "w3_q")
+        w3_sc = held([P, N], U8, "w3_sc")
+        nc.vector.quantize_mx(w3_q[:].bitcast(FP8X4), w3_sc[:], w3_bf[:].rearrange("p n j -> p (n j)"))
+
+        x_q = [held([P, BANK], U32, "x_q%d" % c) for c in range(chunks)]
+        x_sc = [held([P, BANK], U8, "x_sc%d" % c) for c in range(chunks)]
+        for c in range(chunks):
+            got = held([P, PACK, BANK], F32, "got%d" % c, "slot_e%d" % c)
+            for t in range(PACK):
+                nc.vector.tensor_copy(got[:, t, :], page[t][:].indirect(fetch[:, 32 * c : 32 * (c + 1)]))
+            x_bf = ring.tile([P, BANK, PACK], BF16, name="x_bf", align_bytes=ALIGN)
+            nc.vector.tensor_tensor(
+                x_bf[:].rearrange("p (c i) t -> p c t i", i=4),
+                got[:].rearrange("p t (c i) -> p c t i", i=4),
+                sat_sb[c][:].rearrange("p t (c i) -> p c t i", i=4),
+                MIN,
+            )
+            nc.vector.quantize_mx(x_q[c][:].bitcast(FP8X4), x_sc[c][:], x_bf[:].rearrange("p m t -> p (m t)"))
+
+        for c in range(chunks):
+            for b in range(N // P):
+                rows = slice(P * b, P * (b + 1))
+                y2 = psum.tile([P, BANK], F32, name="y2", tag="mx")
+                nc.tensor.matmul_mx(
+                    y2[:], lhsT=w3_q[:, rows].bitcast(FP8X4), lhsT_scale=w3_sc[:, rows],
+                    rhs=x_q[c][:].bitcast(FP8X4), rhs_scale=x_sc[c][:], start=True, stop=True,
+                )
+                y1 = psum.tile([P, BANK], F32, name="y1", tag="plain")
+                nc.tensor.matmul_mx(
+                    y1[:], lhsT=w4_q[:, 2 * P * b : 2 * P * (b + 1)].bitcast(FP4X4), lhsT_scale=w4_sc[:, rows],
+                    rhs=x_q[c][:].bitcast(FP8X4), rhs_scale=x_sc[c][:], start=True, stop=True,
+                )
+                gated = ring.tile([P, BANK], F32, name="gated")
+                nc.vector.tensor_tensor(gated[:], y2[:], slu[c][:, b, :], MULT)
+                y = ring.tile([P, BANK], F32, name="y", bufs=4)
+                nc.vector.tensor_tensor(y[:], y1[:], gated[:], ADD)
+                nc.sync.dma_start(out_0[rows, BANK * c : BANK * (c + 1)], y[:])
+
+        codes = held([P, T2], I32, "codes")
+        scales = held([P, T2], U8, "scales")
+        words_out = out_2[0].rearrange("p m t -> p (m t)").bitcast(I32)
+        for u in range(T2 // BANK):
+            cols = slice(BANK * u, BANK * (u + 1))
+            woven = held([P, BANK, PACK], BF16, "woven%d" % u, "slot_c%d" % u)
+            src = page_bf[u // 2][:, :, BANK * (u % 2) : BANK * (u % 2 + 1)]
+            nc.scalar.copy(woven[:].rearrange("p (c i) t -> p c t i", i=4), src.rearrange("p t (c i) -> p c t i", i=4))
+            nc.vector.quantize_mx(codes[:, cols].bitcast(FP8X4), scales[:, cols], woven[:].rearrange("p m t -> p (m t)"))
+            if u % 2 == 1:
+                both = slice(BANK * (u - 1), BANK * (u + 1))
+                nc.sync.dma_start(words_out[:, both], codes[:, both])
+        for q in range(4):
+            nc.sync.dma_start(out_3[0, 4 * q : 4 * q + 4, :].bitcast(I32), scales[32 * q : 32 * q + 4, :].bitcast(I32))

@@ -33,11 +33,15 @@ def tile_list_brine_pond_page_kernel(
     with ExitStack() as ctx:
         lists = ctx.enter_context(tc.tile_pool(name="lists", bufs=1))
         keep = ctx.enter_context(tc.tile_pool(name="keep", bufs=1))
+        shared = ctx.enter_context(tc.tile_pool(name="shared", bufs=1))
         ring = ctx.enter_context(tc.tile_pool(name="ring", bufs=2))
         psum = ctx.enter_context(tc.psum_pool(name="psum", bufs=4))
 
         def held(shape, dtype, name, tag=None):
             return keep.tile(shape, dtype, name=name, tag=tag or name, align_bytes=ALIGN)
+
+        def placed(shape, dtype, name, kib):
+            return shared.tile(shape, dtype, name=name, align_bytes=ALIGN, offset=1024 * kib)
 
         pick = lists.tile([P, S // 16], U16, name="pick")
         put = lists.tile([P, S // 16], U16, name="put")
@@ -45,23 +49,30 @@ def tile_list_brine_pond_page_kernel(
 
         tab_sc = held([P, T], U8, "tab_sc")
         nc.vector.memset(tab_sc[:].bitcast(I32), 0)
-        for q in range(4):
-            nc.scalar.dma_start(
-                tab_sc[32 * q : 32 * q + 4 * PASSES, :].bitcast(I32), tab_scales[:, 4 * q : 4 * q + 4, :].bitcast(I32)
-            )
         wgs_rows = held([P, S], F32, "wgs_rows")
         nc.sync.dma_start(pick[:], offs)
         nc.sync.dma_start(wgs_rows[:], wgs)
-        tab = [held([P, T], I32, "tab%d" % a, "slot_a%d" % a) for a in range(PASSES)]
-        w1_raw = [held([P, PACK, H], F32, "w1_raw%d" % a, "slot_b%d" % a) for a in range(PASSES)]
-        for a in range(PASSES):
+        tab = [placed([P, T], I32, "tab%d" % a, 8 * a) for a in range(PASSES)]
+        w1_raw = [placed([P, PACK, H], F32, "w1_raw%d" % a, 25 + 8 * a) for a in range(PASSES)]
+
+        def load_tab(a):
             nc.sync.dma_start(tab[a][:], tab_words[a].rearrange("p t i -> p (t i)").bitcast(I32))
+
+        for a in range(PASSES):
+            if a < PASSES - 1:
+                load_tab(a)
+            if a == 0:
+                for q in range(4):
+                    nc.sync.dma_start(
+                        tab_sc[32 * q : 32 * q + 4 * PASSES, :].bitcast(I32),
+                        tab_scales[:, 4 * q : 4 * q + 4, :].bitcast(I32),
+                    )
             nc.sync.dma_start(w1_raw[a][:], w1[512 * a : 512 * (a + 1), :].rearrange("(p j) r -> p j r", j=PACK))
+        load_tab(PASSES - 1)
 
         ident = held([P, P], F32, "ident")
         make_identity(nc, ident[:])
         vec_sb = held([P, PACK], F32, "vec_sb")
-        nc.gpsimd.dma_start(vec_sb[:], vec.rearrange("(p t) -> p t", t=PACK))
         w4_sc = held([P, N], U8, "w4_sc")
         nc.gpsimd.memset(w4_sc[:].bitcast(I32), 0)
         for q in range(4):
@@ -69,14 +80,18 @@ def tile_list_brine_pond_page_kernel(
 
         weather_rows = weather.rearrange("(p t) j -> t p j", t=PACK)
         page_rows = page0.rearrange("(p t) c -> t p c", t=PACK)
-        wea = [held([P, S], F32, "wea%d" % t, "slot_c%d" % t) for t in range(PACK)]
+        wea = [placed([P, S], F32, "wea%d" % t, 65 + 4 * t) for t in range(PACK)]
         page = [held([P, T2], F32, "page%d" % t) for t in range(PACK)]
+        nc.sync.dma_start(vec_sb[:], vec.rearrange("(p t) -> p t", t=PACK))
         nc.sync.dma_start(put[:], offs2)
-        for t in range(PACK):
+        nc.sync.dma_start(wea[0][:, 0:BANK], weather_rows[0][:, 0:BANK])
+        nc.sync.dma_start(page[0][:], page_rows[0])
+        nc.sync.dma_start(wea[0][:, BANK:S], weather_rows[0][:, BANK:S])
+        for t in range(1, PACK):
             nc.sync.dma_start(wea[t][:], weather_rows[t])
             nc.sync.dma_start(page[t][:], page_rows[t])
 
-        wgs_t = [held([P, 4, PACK, 4, 32], F32, "wgs_t%d" % u, "slot_e%d" % u) for u in range(S // BANK)]
+        wgs_t = [placed([P, 4, PACK, 4, 32], F32, "wgs_t%d" % u, 49 + 8 * u) for u in range(S // BANK)]
         for half in range(S // BANK):
             bank = psum.tile([P, 4, P], F32, name="bank", tag="plain")
             for b in range(4):
@@ -85,7 +100,7 @@ def tile_list_brine_pond_page_kernel(
             for b in range(4):
                 src = bank[:, b, :].rearrange("j (q t) -> j t q", t=PACK).unsqueeze(2).to_broadcast([P, PACK, 4, 32])
                 nc.scalar.copy(wgs_t[half][:, b, :, :, :], src)
-        wgd = [held([P, S], F32, "wgd%d" % t) for t in range(PACK)]
+        wgd = [placed([P, S], F32, "wgd0", 81), held([P, S], F32, "wgd1"), placed([P, S], F32, "wgd2", 41), placed([P, S], F32, "wgd3", 45)]
 
         def deal_wgs(t):
             for half in range(S // BANK):
@@ -97,54 +112,58 @@ def tile_list_brine_pond_page_kernel(
                 nc.scalar.copy(wgd[t][:, BANK * half : BANK * (half + 1)], bank[:].rearrange("p b j -> p (b j)"))
 
         deal_wgs(0)
+        deal_wgs(1)
 
-        v_words = [held([P, S], U32, "v_words%d" % a) for a in range(PASSES)]
-        v_sc = held([P, S], U8, "v_sc")
+        halves = S // BANK
+        v_whole = [held([P, S], U32, "v_words%d" % a) for a in range(PASSES - 1)]
+        v_last = [placed([P, BANK], U32, "v_last%d" % u, 49 - 16 * u) for u in range(halves)]
+        v_sc = placed([P, S], U8, "v_sc", 57)
         w1_q = [held([P, H], U32, "w1_q%d" % a) for a in range(PASSES)]
         w1_sc = [held([P, H], U8, "w1_sc%d" % a) for a in range(PASSES)]
+        w1_bf = [
+            held([P, PACK, P, PACK], BF16, "w1_bf0", "slot_d0"),
+            placed([P, PACK, P, PACK], BF16, "w1_bf1", 49),
+            placed([P, PACK, P, PACK], BF16, "w1_bf2", 33),
+        ]
         for a in range(PASSES):
-            nc.vector.tensor_copy(v_words[a][:], tab[a][:].bitcast(U32).indirect(pick[:]))
-            if a == 0:
+            if a < PASSES - 1:
+                nc.vector.tensor_copy(v_whole[a][:], tab[a][:].bitcast(U32).indirect(pick[:]))
+            if a == 1:
                 nc.vector.tensor_copy(v_sc[:], tab_sc[:].indirect(pick[:]))
             dealt = w1_raw[a][:].rearrange("p j (m t) -> p m t j", t=PACK)
-            if a < PASSES - 1:
-                grouped = held([P, PACK, P, PACK], BF16, "w1_bf%d" % a, "slot_d%d" % a)
-                nc.scalar.copy(grouped[:].rearrange("p t m j -> p m t j"), dealt)
-                nc.vector.quantize_mx(w1_q[a][:].bitcast(FP8X4), w1_sc[a][:], grouped[:].rearrange("p t m j -> p (t m j)"))
-            else:
-                first = held([P, P, PACK], BF16, "w1_bf_first")
-                nc.vector.tensor_copy(first[:], dealt[:, :, 0, :])
-                nc.vector.quantize_mx(
-                    w1_q[a][:, 0:P].bitcast(FP8X4), w1_sc[a][:, 0:P], first[:].rearrange("p m j -> p (m j)")
+            cast = nc.vector.tensor_copy if a == 0 else nc.scalar.copy
+            cast(w1_bf[a][:].rearrange("p t m j -> p m t j"), dealt)
+            nc.vector.quantize_mx(w1_q[a][:].bitcast(FP8X4), w1_sc[a][:], w1_bf[a][:].rearrange("p t m j -> p (t m j)"))
+            if a > 0:
+                u = a - 1
+                nc.vector.tensor_copy(
+                    v_last[u][:], tab[PASSES - 1][:].bitcast(U32).indirect(pick[:, 32 * u : 32 * (u + 1)])
                 )
-                rest = held([P, PACK - 1, P, PACK], BF16, "w1_bf_rest")
-                nc.scalar.copy(rest[:].rearrange("p t m j -> p m t j"), dealt[:, :, 1:PACK, :])
-                for t in range(1, PACK):
-                    cols = slice(P * t, P * (t + 1))
-                    nc.vector.quantize_mx(
-                        w1_q[a][:, cols].bitcast(FP8X4), w1_sc[a][:, cols], rest[:, t - 1, :, :].rearrange("p m j -> p (m j)")
-                    )
-        for t in range(1, PACK):
-            deal_wgs(t)
+        deal_wgs(2)
+        deal_wgs(3)
+
+        def v_words(a, half):
+            if a == PASSES - 1:
+                return v_last[half][:]
+            return v_whole[a][:, BANK * half : BANK * (half + 1)]
 
         chunks = M // BANK
         nc.sync.dma_start(fetch[:], offs3)
-        w3_raw = held([P, PACK, N], F32, "w3_raw", "slot_a2")
+        w3_raw = placed([P, PACK, N], F32, "w3_raw", 0)
         nc.sync.dma_start(w3_raw[:], w3.rearrange("(p j) n -> p j n", j=PACK))
         w4_q = held([P, 2 * N], U8, "w4_q")
         nc.sync.dma_start(w4_q[:].bitcast(I32), w4_words[0].bitcast(I32))
-        sat_sb = [held([P, PACK, BANK], F32, "sat%d" % c, "slot_a%d" % c) for c in range(chunks)]
-        slu = [held([P, N // P, BANK], F32, "slu%d" % c, "slot_b%d" % c) for c in range(chunks)]
+        sat_sb = [placed([P, PACK, BANK], F32, "sat%d" % c, 9 + 8 * c) for c in range(chunks)]
+        slu = [placed([P, N // P, BANK], F32, "slu0", 65), placed([P, N // P, BANK], F32, "slu1", 25)]
+        slu_rows = sluice.rearrange("(b p) m -> p b m", p=P)
+        sat_rows = sat.rearrange("(p t) m -> p t m", t=PACK)
         for c in range(chunks):
-            cols = slice(BANK * c, BANK * (c + 1))
-            nc.sync.dma_start(sat_sb[c][:], sat[:, cols].rearrange("(p t) m -> p t m", t=PACK))
-            nc.sync.dma_start(slu[c][:], sluice[:, cols].rearrange("(b p) m -> p b m", p=P))
+            nc.sync.dma_start(sat_sb[c][:], sat_rows[:, :, BANK * c : BANK * (c + 1)])
+        nc.sync.dma_start(slu[1][:], slu_rows[:, :, BANK:M])
 
         out_rows = out_1.rearrange("(p t) c -> t p c", t=PACK)
-        page_bf = [
-            held([P, PACK, T2 // 2], BF16, "page_bf0", "slot_b2"),
-            held([P, PACK, T2 // 2], BF16, "page_bf1"),
-        ]
+        woven = [held([P, T2 // 2, PACK], BF16, "woven0"), held([P, T2 // 2, PACK], BF16, "woven1")]
+        got = [placed([P, PACK, BANK], F32, "got%d" % c, 49 + 8 * c) for c in range(chunks)]
         for t in range(PACK):
             h = ring.tile([P, S], F32, name="h")
             rows = slice(P * t, P * (t + 1))
@@ -154,68 +173,116 @@ def tile_list_brine_pond_page_kernel(
                 for a in range(PASSES):
                     nc.tensor.matmul_mx(
                         acc[:], lhsT=w1_q[a][:, rows].bitcast(FP8X4), lhsT_scale=w1_sc[a][:, rows],
-                        rhs=v_words[a][:, cols].bitcast(FP8X4), rhs_scale=v_sc[4 * a : P, cols],
+                        rhs=v_words(a, half).bitcast(FP8X4), rhs_scale=v_sc[4 * a : P, cols],
                         start=(a == 0), stop=(a == PASSES - 1),
                     )
                 nc.vector.scalar_tensor_tensor(h[:, cols], acc[:], vec_sb[:, t : t + 1], wea[t][:, cols], MULT, ADD)
-            nc.vector.tensor_tensor(page[t][:].indirect(put[:]), h[:], wgd[t][:], MULT)
+            if t == 0:
+                for half in range(S // BANK):
+                    cols = slice(BANK * half, BANK * (half + 1))
+                    nc.vector.tensor_tensor(
+                        page[t][:].indirect(put[:, 32 * half : 32 * (half + 1)]), h[:, cols], wgd[t][:, cols], MULT
+                    )
+            else:
+                nc.vector.tensor_tensor(page[t][:].indirect(put[:]), h[:], wgd[t][:], MULT)
             nc.sync.dma_start(out_rows[t], page[t][:])
-            for u in range(2):
-                nc.scalar.copy(page_bf[u][:, t, :], page[t][:, 1024 * u : 1024 * (u + 1)])
-
-        w3_bf = held([P, N, PACK], BF16, "w3_bf", "slot_d0")
-        nc.scalar.copy(
-            w3_bf[:].rearrange("p (c i) j -> p c j i", i=4), w3_raw[:].rearrange("p j (c i) -> p c j i", i=4)
-        )
-        w3_q = held([P, N], U32, "w3_q")
-        w3_sc = held([P, N], U8, "w3_sc")
-        nc.vector.quantize_mx(w3_q[:].bitcast(FP8X4), w3_sc[:], w3_bf[:].rearrange("p n j -> p (n j)"))
+            for u in range(4):
+                nc.scalar.copy(
+                    woven[u // 2][:, BANK * (u % 2) : BANK * (u % 2 + 1), t], page[t][:, BANK * u : BANK * (u + 1)]
+                )
+            if t == 0:
+                w3_bf = placed([P, N, PACK], BF16, "w3_bf", 81)
+                nc.scalar.copy(
+                    w3_bf[:].rearrange("p (c i) j -> p c j i", i=4), w3_raw[:].rearrange("p j (c i) -> p c j i", i=4)
+                )
+            if t == 1:
+                nc.sync.dma_start(slu[0][:], slu_rows[:, :, 0:BANK])
+            if t == 2:
+                slu_t = placed([P, 4, N], F32, "slu_t", 33)
+                for mb in range(4):
+                    bank = psum.tile([P, N // P, P], F32, name="bank", tag="plain")
+                    for b in range(N // P):
+                        nc.tensor.transpose(bank[:, b, :], slu[0][:, b, P * mb : P * (mb + 1)], ident[:])
+                    nc.scalar.copy(slu_t[:, mb, :], bank[:].rearrange("m b p -> m (b p)"))
+            if t == 3:
+                w3_q = placed([P, N], U32, "w3_q", 77)
+                w3_sc = placed([P, N], U8, "w3_sc", 79)
+                nc.vector.quantize_mx(w3_q[:].bitcast(FP8X4), w3_sc[:], w3_bf[:].rearrange("p n j -> p (n j)"))
 
         x_q = [held([P, BANK], U32, "x_q%d" % c) for c in range(chunks)]
         x_sc = [held([P, BANK], U8, "x_sc%d" % c) for c in range(chunks)]
         for c in range(chunks):
-            got = held([P, PACK, BANK], F32, "got%d" % c, "slot_e%d" % c)
             for t in range(PACK):
-                nc.vector.tensor_copy(got[:, t, :], page[t][:].indirect(fetch[:, 32 * c : 32 * (c + 1)]))
+                nc.vector.tensor_copy(got[c][:, t, :], page[t][:].indirect(fetch[:, 32 * c : 32 * (c + 1)]))
             x_bf = ring.tile([P, BANK, PACK], BF16, name="x_bf", align_bytes=ALIGN)
             nc.vector.tensor_tensor(
                 x_bf[:].rearrange("p (c i) t -> p c t i", i=4),
-                got[:].rearrange("p t (c i) -> p c t i", i=4),
+                got[c][:].rearrange("p t (c i) -> p c t i", i=4),
                 sat_sb[c][:].rearrange("p t (c i) -> p c t i", i=4),
                 MIN,
             )
             nc.vector.quantize_mx(x_q[c][:].bitcast(FP8X4), x_sc[c][:], x_bf[:].rearrange("p m t -> p (m t)"))
 
-        for c in range(chunks):
+        y0 = placed([P, N // P, BANK], F32, "y0", 41)
+        y2_t, y1_t, gated_t = [], [], []
+        for mb in range(4):
+            cols = slice(P * mb, P * (mb + 1))
+            y2 = psum.tile([P, N], F32, name="y2", tag="mx")
+            nc.tensor.matmul_mx(
+                y2[:], lhsT=x_q[0][:, cols].bitcast(FP8X4), lhsT_scale=x_sc[0][:, cols],
+                rhs=w3_q[:].bitcast(FP8X4), rhs_scale=w3_sc[:], start=True, stop=True,
+            )
+            y2_t.append(y2)
+            y1 = psum.tile([P, N], F32, name="y1", tag="plain")
+            nc.tensor.matmul_mx(
+                y1[:], lhsT=x_q[0][:, cols].bitcast(FP8X4), lhsT_scale=x_sc[0][:, cols],
+                rhs=w4_q[:].bitcast(FP4X4), rhs_scale=w4_sc[:], start=True, stop=True,
+            )
+            y1_t.append(ring.tile([P, N], F32, name="y1_t", bufs=4))
+            nc.scalar.copy(y1_t[mb][:], y1[:])
+        sums = []
+        for mb in range(4):
+            sums.append(psum.tile([P, N // P, P], F32, name="bank", tag="plain"))
             for b in range(N // P):
-                rows = slice(P * b, P * (b + 1))
-                y2 = psum.tile([P, BANK], F32, name="y2", tag="mx")
-                nc.tensor.matmul_mx(
-                    y2[:], lhsT=w3_q[:, rows].bitcast(FP8X4), lhsT_scale=w3_sc[:, rows],
-                    rhs=x_q[c][:].bitcast(FP8X4), rhs_scale=x_sc[c][:], start=True, stop=True,
+                nc.tensor.matmul(
+                    sums[mb][:, b, :], lhsT=y1_t[mb][:, P * b : P * (b + 1)], rhs=ident[:],
+                    start=(b == 0), stop=False, is_transpose=True,
                 )
-                y1 = psum.tile([P, BANK], F32, name="y1", tag="plain")
-                nc.tensor.matmul_mx(
-                    y1[:], lhsT=w4_q[:, 2 * P * b : 2 * P * (b + 1)].bitcast(FP4X4), lhsT_scale=w4_sc[:, rows],
-                    rhs=x_q[c][:].bitcast(FP8X4), rhs_scale=x_sc[c][:], start=True, stop=True,
+        for mb in range(4):
+            gated_t.append(placed([P, N], F32, "gated_t%d" % mb, 65 + 2 * mb))
+            nc.vector.tensor_tensor(gated_t[mb][:], y2_t[mb][:], slu_t[:, mb, :], MULT)
+            for b in range(N // P):
+                nc.tensor.matmul(
+                    sums[mb][:, b, :], lhsT=gated_t[mb][:, P * b : P * (b + 1)], rhs=ident[:],
+                    start=False, stop=(b == N // P - 1), is_transpose=True,
                 )
-                gated = ring.tile([P, BANK], F32, name="gated")
-                nc.vector.tensor_tensor(gated[:], y2[:], slu[c][:, b, :], MULT)
-                y = ring.tile([P, BANK], F32, name="y", bufs=4)
-                nc.vector.tensor_tensor(y[:], y1[:], gated[:], ADD)
-                nc.sync.dma_start(out_0[rows, BANK * c : BANK * (c + 1)], y[:])
+            nc.scalar.copy(y0[:, :, P * mb : P * (mb + 1)], sums[mb][:])
+        nc.sync.dma_start(out_0.rearrange("(b p) m -> p b m", p=P)[:, :, 0:BANK], y0[:])
 
         codes = held([P, T2], I32, "codes")
         scales = held([P, T2], U8, "scales")
         words_out = out_2[0].rearrange("p m t -> p (m t)").bitcast(I32)
-        for u in range(T2 // BANK):
-            cols = slice(BANK * u, BANK * (u + 1))
-            woven = held([P, BANK, PACK], BF16, "woven%d" % u, "slot_c%d" % u)
-            src = page_bf[u // 2][:, :, BANK * (u % 2) : BANK * (u % 2 + 1)]
-            nc.scalar.copy(woven[:].rearrange("p (c i) t -> p c t i", i=4), src.rearrange("p t (c i) -> p c t i", i=4))
-            nc.vector.quantize_mx(codes[:, cols].bitcast(FP8X4), scales[:, cols], woven[:].rearrange("p m t -> p (m t)"))
-            if u % 2 == 1:
-                both = slice(BANK * (u - 1), BANK * (u + 1))
-                nc.sync.dma_start(words_out[:, both], codes[:, both])
+        for u in range(2):
+            cols = slice(1024 * u, 1024 * (u + 1))
+            nc.vector.quantize_mx(codes[:, cols].bitcast(FP8X4), scales[:, cols], woven[u][:].rearrange("p m t -> p (m t)"))
+            nc.sync.dma_start(words_out[:, cols], codes[:, cols])
         for q in range(4):
             nc.sync.dma_start(out_3[0, 4 * q : 4 * q + 4, :].bitcast(I32), scales[32 * q : 32 * q + 4, :].bitcast(I32))
+
+        for b in range(N // P):
+            rows = slice(P * b, P * (b + 1))
+            y2 = psum.tile([P, BANK], F32, name="y2", tag="mx")
+            nc.tensor.matmul_mx(
+                y2[:], lhsT=w3_q[:, rows].bitcast(FP8X4), lhsT_scale=w3_sc[:, rows],
+                rhs=x_q[1][:].bitcast(FP8X4), rhs_scale=x_sc[1][:], start=True, stop=True,
+            )
+            y1 = psum.tile([P, BANK], F32, name="y1", tag="plain")
+            nc.tensor.matmul_mx(
+                y1[:], lhsT=w4_q[:, 2 * P * b : 2 * P * (b + 1)].bitcast(FP4X4), lhsT_scale=w4_sc[:, rows],
+                rhs=x_q[1][:].bitcast(FP8X4), rhs_scale=x_sc[1][:], start=True, stop=True,
+            )
+            gated = ring.tile([P, BANK], F32, name="gated")
+            nc.vector.tensor_tensor(gated[:], y2[:], slu[1][:, b, :], MULT)
+            y = ring.tile([P, BANK], F32, name="y", bufs=4)
+            nc.vector.tensor_tensor(y[:], y1[:], gated[:], ADD)
+            nc.sync.dma_start(out_0[rows, BANK:M], y[:])

@@ -59,8 +59,7 @@ def tile_list_brine_pond_page_kernel(
             nc.sync.dma_start(tab[a][:], tab_words[a].rearrange("p t i -> p (t i)").bitcast(I32))
 
         for a in range(PASSES):
-            if a < PASSES - 1:
-                load_tab(a)
+            load_tab(a)
             if a == 0:
                 for q in range(4):
                     nc.sync.dma_start(
@@ -68,7 +67,6 @@ def tile_list_brine_pond_page_kernel(
                         tab_scales[:, 4 * q : 4 * q + 4, :].bitcast(I32),
                     )
             nc.sync.dma_start(w1_raw[a][:], w1[512 * a : 512 * (a + 1), :].rearrange("(p j) r -> p j r", j=PACK))
-        load_tab(PASSES - 1)
 
         ident = held([P, P], F32, "ident")
         make_identity(nc, ident[:])
@@ -87,70 +85,88 @@ def tile_list_brine_pond_page_kernel(
         nc.sync.dma_start(wea[0][:, 0:BANK], weather_rows[0][:, 0:BANK])
         nc.sync.dma_start(page[0][:], page_rows[0])
         nc.sync.dma_start(wea[0][:, BANK:S], weather_rows[0][:, BANK:S])
-        for t in range(1, PACK):
+
+        def load_slice(t):
             nc.sync.dma_start(wea[t][:], weather_rows[t])
             nc.sync.dma_start(page[t][:], page_rows[t])
 
-        wgs_t = [placed([P, 4, PACK, 4, 32], F32, "wgs_t%d" % u, 49 + 8 * u) for u in range(S // BANK)]
-        for half in range(S // BANK):
-            bank = psum.tile([P, 4, P], F32, name="bank", tag="plain")
-            for b in range(4):
-                j0 = BANK * half + P * b
-                nc.tensor.transpose(bank[:, b, :], wgs_rows[:, j0 : j0 + P], ident[:])
-            for b in range(4):
-                src = bank[:, b, :].rearrange("j (q t) -> j t q", t=PACK).unsqueeze(2).to_broadcast([P, PACK, 4, 32])
-                nc.scalar.copy(wgs_t[half][:, b, :, :, :], src)
-        wgd = [placed([P, S], F32, "wgd0", 81), held([P, S], F32, "wgd1"), placed([P, S], F32, "wgd2", 41), placed([P, S], F32, "wgd3", 45)]
+        load_slice(1)
+
+        halves = S // BANK
+        wgs_t = [
+            [placed([P, 4, 2, 4, 32], F32, "wgs_t%d_%d" % (pair, u), (49, 41)[pair] + 4 * u) for u in range(halves)]
+            for pair in range(2)
+        ]
+
+        def turn_wgs(pair):
+            for half in range(halves):
+                bank = psum.tile([P, 4, P], F32, name="bank", tag="plain")
+                for b in range(4):
+                    j0 = BANK * half + P * b
+                    nc.tensor.transpose(bank[:, b, :], wgs_rows[:, j0 : j0 + P], ident[:])
+                for b in range(4):
+                    src = bank[:, b, :].rearrange("j (q t) -> j t q", t=PACK)[:, 2 * pair : 2 * pair + 2, :]
+                    nc.scalar.copy(wgs_t[pair][half][:, b, :, :, :], src.unsqueeze(2).to_broadcast([P, 2, 4, 32]))
+
+        turn_wgs(0)
+        wgd_first = [placed([P, BANK], F32, "wgd0_%d" % u, 81 + 2 * u) for u in range(halves)]
+        wgd_later = [placed([P, S], F32, "wgd1", 85), placed([P, S], F32, "wgd2", 57), placed([P, S], F32, "wgd3", 61)]
+
+        def wgd(t, half):
+            if t == 0:
+                return wgd_first[half][:]
+            return wgd_later[t - 1][:, BANK * half : BANK * (half + 1)]
 
         def deal_wgs(t):
-            for half in range(S // BANK):
+            for half in range(halves):
                 bank = psum.tile([P, 4, P], F32, name="bank", tag="plain")
                 for b in range(4):
                     nc.tensor.transpose(
-                        bank[:, b, :], wgs_t[half][:, b, t, :, :].rearrange("j g q -> j (g q)"), ident[:]
+                        bank[:, b, :], wgs_t[t // 2][half][:, b, t % 2, :, :].rearrange("j g q -> j (g q)"), ident[:]
                     )
-                nc.scalar.copy(wgd[t][:, BANK * half : BANK * (half + 1)], bank[:].rearrange("p b j -> p (b j)"))
+                nc.scalar.copy(wgd(t, half), bank[:].rearrange("p b j -> p (b j)"))
 
-        deal_wgs(0)
-        deal_wgs(1)
-
-        halves = S // BANK
-        v_whole = [held([P, S], U32, "v_words%d" % a) for a in range(PASSES - 1)]
-        v_last = [placed([P, BANK], U32, "v_last%d" % u, 49 - 16 * u) for u in range(halves)]
-        v_sc = placed([P, S], U8, "v_sc", 57)
-        w1_q = [held([P, H], U32, "w1_q%d" % a) for a in range(PASSES)]
-        w1_sc = [held([P, H], U8, "w1_sc%d" % a) for a in range(PASSES)]
-        w1_bf = [
-            held([P, PACK, P, PACK], BF16, "w1_bf0", "slot_d0"),
-            placed([P, PACK, P, PACK], BF16, "w1_bf1", 49),
-            placed([P, PACK, P, PACK], BF16, "w1_bf2", 33),
-        ]
-        for a in range(PASSES):
-            if a < PASSES - 1:
-                nc.vector.tensor_copy(v_whole[a][:], tab[a][:].bitcast(U32).indirect(pick[:]))
-            if a == 1:
+        last = PASSES - 1
+        v_words = [held([P, S], U32, "v_words0"), held([P, S], U32, "v_words1"), placed([P, S], U32, "v_words2", 89)]
+        v_sc = held([P, S], U8, "v_sc")
+        w1_q = [held([P, H], U32, "w1_q%d" % a) for a in range(last)]
+        w1_sc = [held([P, H], U8, "w1_sc%d" % a) for a in range(last)]
+        w1_bf = [held([P, PACK, P, PACK], BF16, "w1_bf0"), placed([P, PACK, P, PACK], BF16, "w1_bf1", 89)]
+        dealt = [w1_raw[a][:].rearrange("p j (m t) -> p m t j", t=PACK) for a in range(PASSES)]
+        for a in range(last):
+            nc.vector.tensor_copy(v_words[a][:], tab[a][:].bitcast(U32).indirect(pick[:]))
+            if a == 0:
                 nc.vector.tensor_copy(v_sc[:], tab_sc[:].indirect(pick[:]))
-            dealt = w1_raw[a][:].rearrange("p j (m t) -> p m t j", t=PACK)
-            cast = nc.vector.tensor_copy if a == 0 else nc.scalar.copy
-            cast(w1_bf[a][:].rearrange("p t m j -> p m t j"), dealt)
+            nc.scalar.copy(w1_bf[a][:].rearrange("p t m j -> p m t j"), dealt[a])
+            deal_wgs(a)
             nc.vector.quantize_mx(w1_q[a][:].bitcast(FP8X4), w1_sc[a][:], w1_bf[a][:].rearrange("p t m j -> p (t m j)"))
-            if a > 0:
-                u = a - 1
-                nc.vector.tensor_copy(
-                    v_last[u][:], tab[PASSES - 1][:].bitcast(U32).indirect(pick[:, 32 * u : 32 * (u + 1)])
-                )
+        nc.vector.tensor_copy(v_words[last][:], tab[last][:].bitcast(U32).indirect(pick[:]))
+        first_bf = placed([P, P, PACK], BF16, "first_bf", 16)
+        first_q = held([P, P], U32, "first_q")
+        first_sc = held([P, P], U8, "first_sc")
+        nc.vector.tensor_copy(first_bf[:], dealt[last][:, :, 0, :])
+        nc.vector.quantize_mx(first_q[:].bitcast(FP8X4), first_sc[:], first_bf[:].rearrange("p m j -> p (m j)"))
+        rest_bf = placed([P, PACK - 1, P, PACK], BF16, "rest_bf", 93)
+        nc.scalar.copy(rest_bf[:].rearrange("p t m j -> p m t j"), dealt[last][:, :, 1:PACK, :])
+        rest_q = placed([P, (PACK - 1) * P], U32, "rest_q", 81)
+        rest_sc = held([P, (PACK - 1) * P], U8, "rest_sc")
+        turn_wgs(1)
         deal_wgs(2)
         deal_wgs(3)
 
-        def v_words(a, half):
-            if a == PASSES - 1:
-                return v_last[half][:]
-            return v_whole[a][:, BANK * half : BANK * (half + 1)]
+        def w1_operand(a, t):
+            if a < last:
+                return w1_q[a][:, P * t : P * (t + 1)], w1_sc[a][:, P * t : P * (t + 1)]
+            if t == 0:
+                return first_q[:], first_sc[:]
+            return rest_q[:, P * (t - 1) : P * t], rest_sc[:, P * (t - 1) : P * t]
 
         chunks = M // BANK
-        nc.sync.dma_start(fetch[:], offs3)
         w3_raw = placed([P, PACK, N], F32, "w3_raw", 0)
         nc.sync.dma_start(w3_raw[:], w3.rearrange("(p j) n -> p j n", j=PACK))
+        load_slice(2)
+        load_slice(3)
+        nc.sync.dma_start(fetch[:], offs3)
         w4_q = held([P, 2 * N], U8, "w4_q")
         nc.sync.dma_start(w4_q[:].bitcast(I32), w4_words[0].bitcast(I32))
         sat_sb = [placed([P, PACK, BANK], F32, "sat%d" % c, 9 + 8 * c) for c in range(chunks)]
@@ -163,17 +179,17 @@ def tile_list_brine_pond_page_kernel(
 
         out_rows = out_1.rearrange("(p t) c -> t p c", t=PACK)
         woven = [held([P, T2 // 2, PACK], BF16, "woven0"), held([P, T2 // 2, PACK], BF16, "woven1")]
-        got = [placed([P, PACK, BANK], F32, "got%d" % c, 49 + 8 * c) for c in range(chunks)]
+        got = [placed([P, PACK, BANK], F32, "got0", 49), placed([P, PACK, BANK], F32, "got1", 9)]
         for t in range(PACK):
             h = ring.tile([P, S], F32, name="h")
-            rows = slice(P * t, P * (t + 1))
             for half in range(S // BANK):
                 cols = slice(BANK * half, BANK * (half + 1))
                 acc = psum.tile([P, BANK], F32, name="acc", tag="mx")
                 for a in range(PASSES):
+                    codes_a, scales_a = w1_operand(a, t)
                     nc.tensor.matmul_mx(
-                        acc[:], lhsT=w1_q[a][:, rows].bitcast(FP8X4), lhsT_scale=w1_sc[a][:, rows],
-                        rhs=v_words(a, half).bitcast(FP8X4), rhs_scale=v_sc[4 * a : P, cols],
+                        acc[:], lhsT=codes_a.bitcast(FP8X4), lhsT_scale=scales_a,
+                        rhs=v_words[a][:, cols].bitcast(FP8X4), rhs_scale=v_sc[4 * a : P, cols],
                         start=(a == 0), stop=(a == PASSES - 1),
                     )
                 nc.vector.scalar_tensor_tensor(h[:, cols], acc[:], vec_sb[:, t : t + 1], wea[t][:, cols], MULT, ADD)
@@ -181,19 +197,25 @@ def tile_list_brine_pond_page_kernel(
                 for half in range(S // BANK):
                     cols = slice(BANK * half, BANK * (half + 1))
                     nc.vector.tensor_tensor(
-                        page[t][:].indirect(put[:, 32 * half : 32 * (half + 1)]), h[:, cols], wgd[t][:, cols], MULT
+                        page[t][:].indirect(put[:, 32 * half : 32 * (half + 1)]), h[:, cols], wgd(t, half), MULT
                     )
+                    if half == 0:
+                        for lo, hi in ((0, 2), (2, 3)):
+                            nc.vector.quantize_mx(
+                                rest_q[:, P * lo : P * hi].bitcast(FP8X4), rest_sc[:, P * lo : P * hi],
+                                rest_bf[:, lo:hi, :, :].rearrange("p t m j -> p (t m j)"),
+                            )
             else:
-                nc.vector.tensor_tensor(page[t][:].indirect(put[:]), h[:], wgd[t][:], MULT)
+                nc.vector.tensor_tensor(page[t][:].indirect(put[:]), h[:], wgd_later[t - 1][:], MULT)
+            if t == 0:
+                w3_bf = placed([P, N, PACK], BF16, "w3_bf", 93)
+                nc.scalar.copy(
+                    w3_bf[:].rearrange("p (c i) j -> p c j i", i=2), w3_raw[:].rearrange("p j (c i) -> p c j i", i=2)
+                )
             nc.sync.dma_start(out_rows[t], page[t][:])
             for u in range(4):
                 nc.scalar.copy(
                     woven[u // 2][:, BANK * (u % 2) : BANK * (u % 2 + 1), t], page[t][:, BANK * u : BANK * (u + 1)]
-                )
-            if t == 0:
-                w3_bf = placed([P, N, PACK], BF16, "w3_bf", 81)
-                nc.scalar.copy(
-                    w3_bf[:].rearrange("p (c i) j -> p c j i", i=4), w3_raw[:].rearrange("p j (c i) -> p c j i", i=4)
                 )
             if t == 1:
                 nc.sync.dma_start(slu[0][:], slu_rows[:, :, 0:BANK])
@@ -204,24 +226,31 @@ def tile_list_brine_pond_page_kernel(
                     for b in range(N // P):
                         nc.tensor.transpose(bank[:, b, :], slu[0][:, b, P * mb : P * (mb + 1)], ident[:])
                     nc.scalar.copy(slu_t[:, mb, :], bank[:].rearrange("m b p -> m (b p)"))
-            if t == 3:
-                w3_q = placed([P, N], U32, "w3_q", 77)
-                w3_sc = placed([P, N], U8, "w3_sc", 79)
+            if t == 2:
+                w3_q = placed([P, N], U32, "w3_q", 57)
+                w3_sc = placed([P, N], U8, "w3_sc", 59)
                 nc.vector.quantize_mx(w3_q[:].bitcast(FP8X4), w3_sc[:], w3_bf[:].rearrange("p n j -> p (n j)"))
 
         x_q = [held([P, BANK], U32, "x_q%d" % c) for c in range(chunks)]
         x_sc = [held([P, BANK], U8, "x_sc%d" % c) for c in range(chunks)]
-        for c in range(chunks):
+        x_bf = [held([P, BANK, PACK], BF16, "x_bf0"), placed([P, BANK, PACK], BF16, "x_bf1", 33)]
+
+        def fetch_x(c):
             for t in range(PACK):
                 nc.vector.tensor_copy(got[c][:, t, :], page[t][:].indirect(fetch[:, 32 * c : 32 * (c + 1)]))
-            x_bf = ring.tile([P, BANK, PACK], BF16, name="x_bf", align_bytes=ALIGN)
+
+        def quantise_x(c):
             nc.vector.tensor_tensor(
-                x_bf[:].rearrange("p (c i) t -> p c t i", i=4),
-                got[c][:].rearrange("p t (c i) -> p c t i", i=4),
-                sat_sb[c][:].rearrange("p t (c i) -> p c t i", i=4),
+                x_bf[c][:].rearrange("p (c i) t -> p c t i", i=2),
+                got[c][:].rearrange("p t (c i) -> p c t i", i=2),
+                sat_sb[c][:].rearrange("p t (c i) -> p c t i", i=2),
                 MIN,
             )
-            nc.vector.quantize_mx(x_q[c][:].bitcast(FP8X4), x_sc[c][:], x_bf[:].rearrange("p m t -> p (m t)"))
+            nc.vector.quantize_mx(x_q[c][:].bitcast(FP8X4), x_sc[c][:], x_bf[c][:].rearrange("p m t -> p (m t)"))
+
+        fetch_x(0)
+        quantise_x(0)
+        fetch_x(1)
 
         y0 = placed([P, N // P, BANK], F32, "y0", 41)
         y2_t, y1_t, gated_t = [], [], []
@@ -233,6 +262,8 @@ def tile_list_brine_pond_page_kernel(
                 rhs=w3_q[:].bitcast(FP8X4), rhs_scale=w3_sc[:], start=True, stop=True,
             )
             y2_t.append(y2)
+        for mb in range(4):
+            cols = slice(P * mb, P * (mb + 1))
             y1 = psum.tile([P, N], F32, name="y1", tag="plain")
             nc.tensor.matmul_mx(
                 y1[:], lhsT=x_q[0][:, cols].bitcast(FP8X4), lhsT_scale=x_sc[0][:, cols],
@@ -259,7 +290,9 @@ def tile_list_brine_pond_page_kernel(
             nc.scalar.copy(y0[:, :, P * mb : P * (mb + 1)], sums[mb][:])
         nc.sync.dma_start(out_0.rearrange("(b p) m -> p b m", p=P)[:, :, 0:BANK], y0[:])
 
-        codes = held([P, T2], I32, "codes")
+        quantise_x(1)
+
+        codes = placed([P, T2], I32, "codes", 9)
         scales = held([P, T2], U8, "scales")
         words_out = out_2[0].rearrange("p m t -> p (m t)").bitcast(I32)
         for u in range(2):

from contextlib import ExitStack

import concourse.mybir as mybir
from concourse.masks import make_identity

K, T, S, H, T2, M, N = 1536, 2048, 1024, 512, 2048, 1024, 512
FLOPS = 2 * K * H * S + 2 * 2 * H * N * M

F32 = mybir.dt.float32
BF16 = mybir.dt.bfloat16
I32 = mybir.dt.int32
U32 = mybir.dt.uint32
U16 = mybir.dt.uint16
U8 = mybir.dt.uint8
FP8X4 = mybir.dt.float8_e4m3fn_x4
FP4X4 = mybir.dt.float4_e2m1fn_x4
MULT = mybir.AluOpType.mult
ADD = mybir.AluOpType.add
MIN = mybir.AluOpType.min

P = 128
PACK = 4
BANK = 512
PASSES = K // (P * PACK)
ALIGN = 64


def tile_list_brine_pond_page_kernel(
    tc, tab_words, tab_scales, offs, w1, vec, weather, wgs, page0, offs2, offs3, sat, w3, w4_words, w4_scales, sluice,
    out_0, out_1, out_2, out_3,
):
    nc = tc.nc
    with ExitStack() as ctx:
        lists = ctx.enter_context(tc.tile_pool(name="lists", bufs=1))
        keep = ctx.enter_context(tc.tile_pool(name="keep", bufs=1))
        shared = ctx.enter_context(tc.tile_pool(name="shared", bufs=1))
        ring = ctx.enter_context(tc.tile_pool(name="ring", bufs=2))
        psum = ctx.enter_context(tc.psum_pool(name="psum", bufs=4))

        def held(shape, dtype, name, tag=None):
            return keep.tile(shape, dtype, name=name, tag=tag or name, align_bytes=ALIGN)

        def placed(shape, dtype, name, kib):
            return shared.tile(shape, dtype, name=name, align_bytes=ALIGN, offset=1024 * kib)

        pick = lists.tile([P, S // 16], U16, name="pick")
        put = lists.tile([P, S // 16], U16, name="put")
        fetch = lists.tile([P, M // 16], U16, name="fetch")

        tab_sc = held([P, T], U8, "tab_sc")
        nc.vector.memset(tab_sc[:].bitcast(I32), 0)
        wgs_rows = held([P, S], F32, "wgs_rows")
        nc.sync.dma_start(pick[:], offs)
        nc.sync.dma_start(wgs_rows[:], wgs)
        tab = [placed([P, T], I32, "tab%d" % a, 8 * a) for a in range(PASSES)]
        w1_raw = [placed([P, PACK, H], F32, "w1_raw%d" % a, 25 + 8 * a) for a in range(PASSES)]

        def load_tab(a):
            nc.sync.dma_start(tab[a][:], tab_words[a].rearrange("p t i -> p (t i)").bitcast(I32))

        for a in range(PASSES):
            load_tab(a)
            if a == 0:
                for q in range(4):
                    nc.sync.dma_start(
                        tab_sc[32 * q : 32 * q + 4 * PASSES, :].bitcast(I32),
                        tab_scales[:, 4 * q : 4 * q + 4, :].bitcast(I32),
                    )
            nc.sync.dma_start(w1_raw[a][:], w1[512 * a : 512 * (a + 1), :].rearrange("(p j) r -> p j r", j=PACK))

        ident = held([P, P], F32, "ident")
        make_identity(nc, ident[:])
        vec_sb = held([P, PACK], F32, "vec_sb")
        w4_sc = held([P, N], U8, "w4_sc")
        nc.gpsimd.memset(w4_sc[:].bitcast(I32), 0)
        for q in range(4):
            nc.gpsimd.dma_start(w4_sc[32 * q : 32 * q + 4, :].bitcast(I32), w4_scales[0, 4 * q : 4 * q + 4, :].bitcast(I32))

        weather_rows = weather.rearrange("(p t) j -> t p j", t=PACK)
        page_rows = page0.rearrange("(p t) c -> t p c", t=PACK)
        wea = [placed([P, S], F32, "wea%d" % t, 65 + 4 * t) for t in range(PACK)]
        page = [held([P, T2], F32, "page%d" % t) for t in range(PACK)]
        nc.sync.dma_start(vec_sb[:], vec.rearrange("(p t) -> p t", t=PACK))
        nc.sync.dma_start(put[:], offs2)
        nc.sync.dma_start(wea[0][:, 0:BANK], weather_rows[0][:, 0:BANK])
        nc.sync.dma_start(page[0][:], page_rows[0])
        nc.sync.dma_start(wea[0][:, BANK:S], weather_rows[0][:, BANK:S])

        def load_slice(t):
            nc.sync.dma_start(wea[t][:], weather_rows[t])
            nc.sync.dma_start(page[t][:], page_rows[t])

        load_slice(1)

        halves = S // BANK
        wgs_t = [
            [placed([P, 4, 2, 4, 32], F32, "wgs_t%d_%d" % (pair, u), (49, 41)[pair] + 4 * u) for u in range(halves)]
            for pair in range(2)
        ]

        def turn_wgs(pair):
            for half in range(halves):
                bank = psum.tile([P, 4, P], F32, name="bank", tag="plain")
                for b in range(4):
                    j0 = BANK * half + P * b
                    nc.tensor.transpose(bank[:, b, :], wgs_rows[:, j0 : j0 + P], ident[:])
                for b in range(4):
                    src = bank[:, b, :].rearrange("j (q t) -> j t q", t=PACK)[:, 2 * pair : 2 * pair + 2, :]
                    nc.scalar.copy(wgs_t[pair][half][:, b, :, :, :], src.unsqueeze(2).to_broadcast([P, 2, 4, 32]))

        turn_wgs(0)
        wgd_first = [placed([P, BANK], F32, "wgd0_%d" % u, 81 + 2 * u) for u in range(halves)]
        wgd_later = [placed([P, S], F32, "wgd1", 85), placed([P, S], F32, "wgd2", 57), placed([P, S], F32, "wgd3", 61)]

        def wgd(t, half):
            if t == 0:
                return wgd_first[half][:]
            return wgd_later[t - 1][:, BANK * half : BANK * (half + 1)]

        def deal_wgs(t):
            for half in range(halves):
                bank = psum.tile([P, 4, P], F32, name="bank", tag="plain")
                for b in range(4):
                    nc.tensor.transpose(
                        bank[:, b, :], wgs_t[t // 2][half][:, b, t % 2, :, :].rearrange("j g q -> j (g q)"), ident[:]
                    )
                nc.scalar.copy(wgd(t, half), bank[:].rearrange("p b j -> p (b j)"))

        last = PASSES - 1
        v_words = [held([P, S], U32, "v_words0"), held([P, S], U32, "v_words1"), placed([P, S], U32, "v_words2", 89)]
        v_sc = held([P, S], U8, "v_sc")
        w1_q = [held([P, H], U32, "w1_q%d" % a) for a in range(last)]
        w1_sc = [held([P, H], U8, "w1_sc%d" % a) for a in range(last)]
        w1_bf = [held([P, PACK, P, PACK], BF16, "w1_bf0"), placed([P, PACK, P, PACK], BF16, "w1_bf1", 89)]
        dealt = [w1_raw[a][:].rearrange("p j (m t) -> p m t j", t=PACK) for a in range(PASSES)]
        for a in range(last):
            nc.vector.tensor_copy(v_words[a][:], tab[a][:].bitcast(U32).indirect(pick[:]))
            if a == 0:
                nc.vector.tensor_copy(v_sc[:], tab_sc[:].indirect(pick[:]))
            nc.scalar.copy(w1_bf[a][:].rearrange("p t m j -> p m t j"), dealt[a])
            deal_wgs(a)
            nc.vector.quantize_mx(w1_q[a][:].bitcast(FP8X4), w1_sc[a][:], w1_bf[a][:].rearrange("p t m j -> p (t m j)"))
        nc.vector.tensor_copy(v_words[last][:], tab[last][:].bitcast(U32).indirect(pick[:]))
        first_bf = placed([P, P, PACK], BF16, "first_bf", 16)
        first_q = held([P, P], U32, "first_q")
        first_sc = held([P, P], U8, "first_sc")
        nc.vector.tensor_copy(first_bf[:], dealt[last][:, :, 0, :])
        nc.vector.quantize_mx(first_q[:].bitcast(FP8X4), first_sc[:], first_bf[:].rearrange("p m j -> p (m j)"))
        rest_bf = placed([P, PACK - 1, P, PACK], BF16, "rest_bf", 93)
        nc.scalar.copy(rest_bf[:].rearrange("p t m j -> p m t j"), dealt[last][:, :, 1:PACK, :])
        rest_q = placed([P, (PACK - 1) * P], U32, "rest_q", 81)
        rest_sc = held([P, (PACK - 1) * P], U8, "rest_sc")
        turn_wgs(1)
        deal_wgs(2)
        deal_wgs(3)

        def w1_operand(a, t):
            if a < last:
                return w1_q[a][:, P * t : P * (t + 1)], w1_sc[a][:, P * t : P * (t + 1)]
            if t == 0:
                return first_q[:], first_sc[:]
            return rest_q[:, P * (t - 1) : P * t], rest_sc[:, P * (t - 1) : P * t]

        chunks = M // BANK
        w3_raw = placed([P, PACK, N], F32, "w3_raw", 0)
        nc.sync.dma_start(w3_raw[:], w3.rearrange("(p j) n -> p j n", j=PACK))
        load_slice(2)
        load_slice(3)
        nc.sync.dma_start(fetch[:], offs3)
        w4_q = held([P, 2 * N], U8, "w4_q")
        nc.sync.dma_start(w4_q[:].bitcast(I32), w4_words[0].bitcast(I32))
        sat_sb = [placed([P, PACK, BANK], F32, "sat%d" % c, 9 + 8 * c) for c in range(chunks)]
        slu = [placed([P, N // P, BANK], F32, "slu0", 65), placed([P, N // P, BANK], F32, "slu1", 25)]
        slu_rows = sluice.rearrange("(b p) m -> p b m", p=P)
        sat_rows = sat.rearrange("(p t) m -> p t m", t=PACK)
        for c in range(chunks):
            nc.sync.dma_start(sat_sb[c][:], sat_rows[:, :, BANK * c : BANK * (c + 1)])
        nc.sync.dma_start(slu[1][:], slu_rows[:, :, BANK:M])

        out_rows = out_1.rearrange("(p t) c -> t p c", t=PACK)
        woven = [held([P, T2 // 2, PACK], BF16, "woven0"), held([P, T2 // 2, PACK], BF16, "woven1")]
        got = [placed([P, PACK, BANK], F32, "got0", 49), placed([P, PACK, BANK], F32, "got1", 9)]
        for t in range(PACK):
            h = ring.tile([P, S], F32, name="h")
            for half in range(S // BANK):
                cols = slice(BANK * half, BANK * (half + 1))
                acc = psum.tile([P, BANK], F32, name="acc", tag="mx")
                for a in range(PASSES):
                    codes_a, scales_a = w1_operand(a, t)
                    nc.tensor.matmul_mx(
                        acc[:], lhsT=codes_a.bitcast(FP8X4), lhsT_scale=scales_a,
                        rhs=v_words[a][:, cols].bitcast(FP8X4), rhs_scale=v_sc[4 * a : P, cols],
                        start=(a == 0), stop=(a == PASSES - 1),
                    )
                nc.vector.scalar_tensor_tensor(h[:, cols], acc[:], vec_sb[:, t : t + 1], wea[t][:, cols], MULT, ADD)
            if t == 0:
                for half in range(S // BANK):
                    cols = slice(BANK * half, BANK * (half + 1))
                    nc.vector.tensor_tensor(
                        page[t][:].indirect(put[:, 32 * half : 32 * (half + 1)]), h[:, cols], wgd(t, half), MULT
                    )
                    if half == 0:
                        for lo, hi in ((0, 2), (2, 3)):
                            nc.vector.quantize_mx(
                                rest_q[:, P * lo : P * hi].bitcast(FP8X4), rest_sc[:, P * lo : P * hi],
                                rest_bf[:, lo:hi, :, :].rearrange("p t m j -> p (t m j)"),
                            )
            else:
                nc.vector.tensor_tensor(page[t][:].indirect(put[:]), h[:], wgd_later[t - 1][:], MULT)
            if t == 0:
                w3_bf = placed([P, N, PACK], BF16, "w3_bf", 93)
                nc.scalar.copy(
                    w3_bf[:].rearrange("p (c i) j -> p c j i", i=2), w3_raw[:].rearrange("p j (c i) -> p c j i", i=2)
                )
            nc.sync.dma_start(out_rows[t], page[t][:])
            for u in range(4):
                nc.scalar.copy(
                    woven[u // 2][:, BANK * (u % 2) : BANK * (u % 2 + 1), t], page[t][:, BANK * u : BANK * (u + 1)]
                )
            if t == 1:
                nc.sync.dma_start(slu[0][:], slu_rows[:, :, 0:BANK])
            if t == 2:
                slu_t = placed([P, 4, N], F32, "slu_t", 33)
                for mb in range(4):
                    bank = psum.tile([P, N // P, P], F32, name="bank", tag="plain")
                    for b in range(N // P):
                        nc.tensor.transpose(bank[:, b, :], slu[0][:, b, P * mb : P * (mb + 1)], ident[:])
                    nc.scalar.copy(slu_t[:, mb, :], bank[:].rearrange("m b p -> m (b p)"))
            if t == 2:
                w3_q = placed([P, N], U32, "w3_q", 57)
                w3_sc = placed([P, N], U8, "w3_sc", 59)
                nc.vector.quantize_mx(w3_q[:].bitcast(FP8X4), w3_sc[:], w3_bf[:].rearrange("p n j -> p (n j)"))

        x_q = [held([P, BANK], U32, "x_q%d" % c) for c in range(chunks)]
        x_sc = [held([P, BANK], U8, "x_sc%d" % c) for c in range(chunks)]
        x_bf = [held([P, BANK, PACK], BF16, "x_bf0"), placed([P, BANK, PACK], BF16, "x_bf1", 33)]

        def fetch_x(c):
            for t in range(PACK):
                nc.vector.tensor_copy(got[c][:, t, :], page[t][:].indirect(fetch[:, 32 * c : 32 * (c + 1)]))

        def quantise_x(c):
            nc.vector.tensor_tensor(
                x_bf[c][:].rearrange("p (c i) t -> p c t i", i=2),
                got[c][:].rearrange("p t (c i) -> p c t i", i=2),
                sat_sb[c][:].rearrange("p t (c i) -> p c t i", i=2),
                MIN,
            )
            nc.vector.quantize_mx(x_q[c][:].bitcast(FP8X4), x_sc[c][:], x_bf[c][:].rearrange("p m t -> p (m t)"))

        fetch_x(0)
        quantise_x(0)
        fetch_x(1)

        y0 = placed([P, N // P, BANK], F32, "y0", 41)
        y2_t, y1_t, gated_t = [], [], []
        for mb in range(4):
            cols = slice(P * mb, P * (mb + 1))
            y2 = psum.tile([P, N], F32, name="y2", tag="mx")
            nc.tensor.matmul_mx(
                y2[:], lhsT=x_q[0][:, cols].bitcast(FP8X4), lhsT_scale=x_sc[0][:, cols],
                rhs=w3_q[:].bitcast(FP8X4), rhs_scale=w3_sc[:], start=True, stop=True,
            )
            y2_t.append(y2)
        for mb in range(4):
            cols = slice(P * mb, P * (mb + 1))
            y1 = psum.tile([P, N], F32, name="y1", tag="plain")
            nc.tensor.matmul_mx(
                y1[:], lhsT=x_q[0][:, cols].bitcast(FP8X4), lhsT_scale=x_sc[0][:, cols],
                rhs=w4_q[:].bitcast(FP4X4), rhs_scale=w4_sc[:], start=True, stop=True,
            )
            y1_t.append(ring.tile([P, N], F32, name="y1_t", bufs=4))
            nc.scalar.copy(y1_t[mb][:], y1[:])
        sums = []
        for mb in range(4):
            sums.append(psum.tile([P, N // P, P], F32, name="bank", tag="plain"))
            for b in range(N // P):
                nc.tensor.matmul(
                    sums[mb][:, b, :], lhsT=y1_t[mb][:, P * b : P * (b + 1)], rhs=ident[:],
                    start=(b == 0), stop=False, is_transpose=True,
                )
        for mb in range(4):
            gated_t.append(placed([P, N], F32, "gated_t%d" % mb, 65 + 2 * mb))
            nc.vector.tensor_tensor(gated_t[mb][:], y2_t[mb][:], slu_t[:, mb, :], MULT)
            for b in range(N // P):
                nc.tensor.matmul(
                    sums[mb][:, b, :], lhsT=gated_t[mb][:, P * b : P * (b + 1)], rhs=ident[:],
                    start=False, stop=(b == N // P - 1), is_transpose=True,
                )
            nc.scalar.copy(y0[:, :, P * mb : P * (mb + 1)], sums[mb][:])
        nc.sync.dma_start(out_0.rearrange("(b p) m -> p b m", p=P)[:, :, 0:BANK], y0[:])

        quantise_x(1)

        codes = placed([P, T2], I32, "codes", 9)
        scales = held([P, T2], U8, "scales")
        words_out = out_2[0].rearrange("p m t -> p (m t)").bitcast(I32)
        for u in range(2):
            cols = slice(1024 * u, 1024 * (u + 1))
            nc.vector.quantize_mx(codes[:, cols].bitcast(FP8X4), scales[:, cols], woven[u][:].rearrange("p m t -> p (m t)"))
            nc.sync.dma_start(words_out[:, cols], codes[:, cols])
        for q in range(4):
            nc.sync.dma_start(out_3[0, 4 * q : 4 * q + 4, :].bitcast(I32), scales[32 * q : 32 * q + 4, :].bitcast(I32))

        for b in range(N // P):
            rows = slice(P * b, P * (b + 1))
            y2 = psum.tile([P, BANK], F32, name="y2", tag="mx")
            nc.tensor.matmul_mx(
                y2[:], lhsT=w3_q[:, rows].bitcast(FP8X4), lhsT_scale=w3_sc[:, rows],
                rhs=x_q[1][:].bitcast(FP8X4), rhs_scale=x_sc[1][:], start=True, stop=True,
            )
            y1 = psum.tile([P, BANK], F32, name="y1", tag="plain")
            nc.tensor.matmul_mx(
                y1[:], lhsT=w4_q[:, 2 * P * b : 2 * P * (b + 1)].bitcast(FP4X4), lhsT_scale=w4_sc[:, rows],
                rhs=x_q[1][:].bitcast(FP8X4), rhs_scale=x_sc[1][:], start=True, stop=True,
            )
            gated = ring.tile([P, BANK], F32, name="gated")
            nc.vector.tensor_tensor(gated[:], y2[:], slu[1][:, b, :], MULT)
            y = ring.tile([P, BANK], F32, name="y", bufs=4)
            nc.vector.tensor_tensor(y[:], y1[:], gated[:], ADD)
            nc.sync.dma_start(out_0[rows, BANK:M], y[:])
